import numpy as np
import ml_dtypes


def mxq(x, axis, fmt="e4m3"):
    dtype, down = {"e4m3": (ml_dtypes.float8_e4m3fn, 7), "e5m2": (ml_dtypes.float8_e5m2, 14)}[fmt]
    v = np.moveaxis(np.asarray(x, np.float32).astype(ml_dtypes.bfloat16).astype(np.float64), axis, -1)
    blocks = v.reshape(v.shape[:-1] + (-1, 32))
    amax = np.abs(blocks).max(-1, keepdims=True)
    byte = np.maximum(np.where(amax > 0, np.frexp(amax)[1] - 1 + 127, 0) - down, 1)
    scale = np.exp2(byte - 127.0)
    codes = (blocks / scale).astype(np.float32).astype(dtype).astype(np.float64)
    return np.moveaxis((codes * scale).reshape(v.shape), -1, axis)


WIDE = False


def mx_kscale(k):
    if not WIDE:
        return np.ones(k)
    levels = np.array([10, -10, 5, -5, 0])
    if k % 512:
        return np.exp2(np.random.permutation(np.resize(levels, k // 32))).repeat(32)
    a = np.empty((k // 512, 16))
    for p in range(k // 512):
        a[p, :8] = np.random.permutation(np.resize(levels, 8))
        for g in range(8):
            far = levels[np.abs(levels - a[p, g]) >= 10]
            a[p, g + 8] = far[np.random.randint(len(far))]
    return np.exp2(a.ravel()).repeat(32)


def f64(x):
    return np.asarray(x).astype(np.float64)


def striped(idx):
    return np.tile(idx.reshape(-1, 16).T, (8, 1)).astype(np.uint16)


def unstriped(offs):
    return offs[:16].T.reshape(-1).astype(np.int64)


def relu(v):
    return np.maximum(v, 0.0)


K, T, S, D, V, H, N, U = 1024, 2048, 1024, 2, 512, 512, 256, 256
P = 2 ** 7


def setup_inputs():
    n = np.random.standard_normal
    s = mx_kscale(K)[:, None]
    u = mx_kscale(H)
    return {
        "xT": (n((K, T)) * s).astype(np.float32),
        "w1": (n((K, H)) / np.sqrt(K) / s * u).astype(np.float32),
        "w2": (n((H, N)) / np.sqrt(H) / u[:, None]).astype(np.float32),
        "gate": (np.tile(np.random.uniform(0.2, 1.0, (D, 1, V)) / np.sqrt(D), (1, P, 1))).astype(np.float32),
        "gate2": (np.tile(np.random.uniform(0.2, 1.0, (D, 1, U)) / np.sqrt(D), (1, P, 1))).astype(np.float32),
        "offs": striped(np.random.permutation(T)[:S]),
        "pos1": striped(np.random.permutation(S)[:V]),
        "pos2": striped(np.random.permutation(S)[:V]),
        "nxt1": striped(np.random.permutation(V)[:U]),
        "nxt2": striped(np.random.permutation(V)[:U]),
    }


def reference(xT, w1, w2, gate, gate2, offs, pos1, pos2, nxt1, nxt2):
    xq = mxq(f64(xT)[:, unstriped(offs)], 0, "e4m3")
    h = relu(mxq(f64(w1), 0, "e4m3").T @ xq)
    z = h[:, unstriped(pos1)] * f64(gate)[0, :1] + h[:, unstriped(pos2)] * f64(gate)[1, :1]
    g = relu(mxq(f64(w2), 0, "e4m3").T @ mxq(z, 0, "e4m3"))
    return g[:, unstriped(nxt1)] * f64(gate2)[0, :1] + g[:, unstriped(nxt2)] * f64(gate2)[1, :1]

@@ -1,0 +1,195 @@
+from contextlib import ExitStack
+
+import concourse.mybir as mybir
+
+K, T, S, V, H, N, U = 1024, 2048, 1024, 512, 512, 256, 256
+FLOPS = 2 * K * H * S + 2 * H * N * V
+
+F32 = mybir.dt.float32
+BF16 = mybir.dt.bfloat16
+I32 = mybir.dt.int32
+U32 = mybir.dt.uint32
+U16 = mybir.dt.uint16
+U8 = mybir.dt.uint8
+FP8X4 = mybir.dt.float8_e4m3fn_x4
+COPY = mybir.ActivationFunctionType.Copy
+RELU = mybir.ActivationFunctionType.Relu
+MULT = mybir.AluOpType.mult
+ADD = mybir.AluOpType.add
+
+P = 128
+PACK = 4
+K_PASS = P * PACK
+PASSES = K // K_PASS
+BANK = 512
+LIST_ROWS = 16
+
+X_CHUNKS = (
+    (0, 0, 512, 416), (0, 512, 512, 416), (0, 1024, 512, 416), (0, 1536, 512, 416),
+    (1, 0, 512, 448), (1, 512, 512, 448), (1, 1024, 512, 448), (1, 1536, 256, 160), (1, 1792, 256, 96),
+)
+
+
+def tile_picked_hop2_relu_e_kernel(
+    tc, xT, w1, w2, gate, gate2, offs, pos1, pos2, nxt1, nxt2, out
+):
+    nc = tc.nc
+    with ExitStack() as ctx:
+        lists = ctx.enter_context(tc.tile_pool(name="lists", bufs=1))
+        keep = ctx.enter_context(tc.tile_pool(name="keep", bufs=1))
+        psum = ctx.enter_context(tc.psum_pool(name="psum", bufs=1))
+
+        def load_list(name, dram):
+            held = lists.tile(list(dram.shape), U16, name=name)
+            nc.sync.dma_start(held[:], dram)
+            return held
+
+        def mx_tiles(name, width):
+            words = keep.tile([P, width], U32, name=name + "_words", align_bytes=64)
+            scales = keep.tile([P, width], U8, name=name + "_scales", align_bytes=64)
+            return words, scales
+
+        def quantise(words, scales, grouped):
+            nc.vector.quantize_mx(out=words.bitcast(FP8X4), scales=scales, in_=grouped)
+
+        x_all = [mx_tiles("x_all%d" % c, T) for c in range(PASSES)]
+        for c in range(PASSES):
+            nc.vector.memset(x_all[c][1][:].bitcast(I32), 0)
+
+        x_raw = []
+        for n, (c, first, width, share) in enumerate(X_CHUNKS):
+            raw = keep.tile([P, PACK, width], F32, name="x_raw%d" % n)
+            rows = xT[c * K_PASS : (c + 1) * K_PASS, first : first + width]
+            nc.sync.dma_start(raw[:], rows.rearrange("(p j) w -> p j w", j=PACK))
+            x_raw.append(raw)
+            if n == 2:
+                offs_sb = load_list("offs_sb", offs)
+        w1_raw = {}
+        for c in range(PASSES):
+            for half in range(2):
+                raw = keep.tile([P, PACK, H // 2], F32, name="w1_raw%d%d" % (c, half))
+                rows = w1[c * K_PASS : (c + 1) * K_PASS, half * (H // 2) : (half + 1) * (H // 2)]
+                nc.sync.dma_start(raw[:], rows.rearrange("(p j) w -> p j w", j=PACK))
+                w1_raw[c, half] = raw
+        gate_sb = keep.tile([P, 2, V], F32, name="gate_sb")
+        nc.sync.dma_start(gate_sb[:], gate.rearrange("d p v -> p d v"))
+        pos_sb = [load_list("pos1_sb", pos1), load_list("pos2_sb", pos2)]
+        w2_raw = keep.tile([P, PACK, N], F32, name="w2_raw")
+        nc.sync.dma_start(w2_raw[:], w2.rearrange("(p j) w -> p j w", j=PACK))
+        gate2_sb = keep.tile([P, 2, U], F32, name="gate2_sb")
+        nc.sync.dma_start(gate2_sb[:], gate2.rearrange("d p v -> p d v"))
+        nxt_sb = [load_list("nxt1_sb", nxt1), load_list("nxt2_sb", nxt2)]
+
+        def weave_out(ap):
+            return ap.rearrange("p (c i) t -> p c t i", i=PACK)
+
+        def weave_in(ap):
+            return ap.rearrange("p t (c i) -> p c t i", i=PACK)
+
+        def gather(sort, c, half, dtype, tag=""):
+            name = "picked%d%d%d" % (sort, c, half)
+            held = keep.tile([P, BANK], dtype, name=name, align_bytes=64, tag=tag or name)
+            picks = offs_sb[:, half * BANK // LIST_ROWS : (half + 1) * BANK // LIST_ROWS]
+            nc.vector.tensor_copy(held[:], x_all[c][sort][:].indirect(picks))
+            return held
+
+        picked = {}
+        for n, (c, first, width, share) in enumerate(X_CHUNKS):
+            grouped = keep.tile([P, width, PACK], BF16, name="x_grouped%d" % n, align_bytes=64)
+            nc.scalar.activation(weave_out(grouped[:, :share, :]), weave_in(x_raw[n][:, :, :share]), COPY)
+            nc.vector.tensor_copy(weave_out(grouped[:, share:, :]), weave_in(x_raw[n][:, :, share:]))
+            quantise(
+                x_all[c][0][:, first : first + width],
+                x_all[c][1][:, first : first + width],
+                grouped[:].rearrange("p w j -> p (w j)"),
+            )
+            if first + width == T:
+                for half in range(2):
+                    words = gather(0, c, half, U32)
+                    if (c, half) == (PASSES - 1, 1):
+                        last_words = words
+                    else:
+                        picked[c, half] = (words, gather(1, c, half, U8))
+
+        w1_q = {}
+        for c in range(PASSES):
+            grouped = keep.tile([P, PACK, P, PACK], BF16, name="w1_grouped%d" % c, align_bytes=64, tag="w1_grouped%d" % c)
+            for half in range(2):
+                nc.scalar.activation(
+                    grouped[:, :, half * (P // 2) : (half + 1) * (P // 2), :].rearrange("p t m j -> p m j t"),
+                    w1_raw[c, half][:].rearrange("p j (m t) -> p m j t", t=PACK),
+                    COPY,
+                )
+            words, scales = mx_tiles("w1_q%d" % c, H)
+            parts = ((0, 4),) if c == 0 else ((0, 1), (1, 2), (2, 4))
+            for lo, hi in parts:
+                quantise(
+                    words[:, lo * P : hi * P],
+                    scales[:, lo * P : hi * P],
+                    grouped[:, lo:hi, :, :].rearrange("p t m j -> p (t m j)"),
+                )
+            w1_q[c] = (words, scales)
+            if c == 0:
+                picked[PASSES - 1, 1] = (last_words, gather(1, PASSES - 1, 1, U8, tag="w1_grouped0"))
+
+        def product(acc, left, cols, right, start, stop):
+            nc.tensor.matmul_mx(
+                out=acc,
+                lhsT=left[0][:, cols].bitcast(FP8X4),
+                lhsT_scale=left[1][:, cols],
+                rhs=right[0][:].bitcast(FP8X4),
+                rhs_scale=right[1][:],
+                start=start,
+                stop=stop,
+            )
+
+        banks = {}
+        for t in range(PACK):
+            for half in range(2):
+                banks[t, half] = psum.tile([P, BANK], F32, name="h_bank%d%d" % (t, half), tag="bank%d" % (2 * t + half))
+        for t in range(PACK):
+            for c in range(PASSES):
+                for half in range(2):
+                    product(banks[t, half][:], w1_q[c], slice(t * P, (t + 1) * P), picked[c, half], c == 0, c == PASSES - 1)
+
+        w2_grouped = keep.tile([P, N, PACK], BF16, name="w2_grouped", align_bytes=64)
+        nc.vector.tensor_copy(weave_out(w2_grouped[:]), weave_in(w2_raw[:]))
+        w2_q = mx_tiles("w2_q", N)
+        quantise(w2_q[0][:], w2_q[1][:], w2_grouped[:].rearrange("p w j -> p (w j)"))
+
+        terms = [keep.tile([P, PACK, V], F32, name="terms%d" % d) for d in range(2)]
+        for t in range(PACK):
+            h = keep.tile([P, S], F32, name="h%d" % t)
+            nc.scalar.activation(h[:, :BANK], banks[t, 0][:], RELU)
+            if t == 0:
+                nc.vector.tensor_scalar_max(h[:, BANK:], banks[t, 1][:], 0.0)
+            else:
+                nc.scalar.activation(h[:, BANK:], banks[t, 1][:], RELU)
+            for d in range(2):
+                nc.vector.tensor_tensor(terms[d][:, t, :], h[:].indirect(pos_sb[d][:]), gate_sb[:, d, :], MULT)
+
+        z_grouped = []
+        for half in range(2):
+            cols = slice(half * (V // 2), (half + 1) * (V // 2))
+            grouped = keep.tile([P, V // 2, PACK], BF16, name="z_grouped%d" % half, align_bytes=64)
+            nc.vector.tensor_tensor(weave_out(grouped[:]), weave_in(terms[0][:, :, cols]), weave_in(terms[1][:, :, cols]), ADD)
+            z_grouped.append(grouped)
+        g = [keep.tile([P, V], F32, name="g%d" % m) for m in range(N // P)]
+        z_q = []
+        for half in range(2):
+            z_q.append(mx_tiles("z_q%d" % half, V // 2))
+            quantise(z_q[half][0][:], z_q[half][1][:], z_grouped[half][:].rearrange("p w j -> p (w j)"))
+        for half in range(2):
+            cols = slice(half * (V // 2), (half + 1) * (V // 2))
+            for m in range(N // P):
+                acc = psum.tile([P, V // 2], F32, name="g_bank%d%d" % (m, half), tag="bank%d" % (2 * half + m))
+                product(acc[:], w2_q, slice(m * P, (m + 1) * P), z_q[half], True, True)
+                nc.scalar.activation(g[m][:, cols], acc[:], RELU)
+
+        ends = [[keep.tile([P, U], F32, name="ends%d%d" % (m, d)) for d in range(2)] for m in range(N // P)]
+        for m in range(N // P):
+            for d in range(2):
+                nc.vector.tensor_tensor(ends[m][d][:], g[m][:].indirect(nxt_sb[d][:]), gate2_sb[:, d, :], MULT)
+            result = keep.tile([P, U], F32, name="result%d" % m)
+            nc.vector.tensor_tensor(result[:], ends[m][0][:], ends[m][1][:], ADD)
+            nc.sync.dma_start(out[m * P : (m + 1) * P, :], result[:])

@@ -1,6 +1,7 @@
 from contextlib import ExitStack
 
 import concourse.mybir as mybir
+from concourse.masks import make_identity
 
 K, T, S, V, H, N, U = 1024, 2048, 1024, 512, 512, 256, 256
 FLOPS = 2 * K * H * S + 2 * H * N * V
@@ -23,10 +24,22 @@ K_PASS = P * PACK
 PASSES = K // K_PASS
 BANK = 512
 LIST_ROWS = 16
+PLANE_STEP = 4
+TURNED = 2
+G_BANKS = ("bank1", "bank2", "bank3", "bank6")
 
+X_LOADS = (
+    (0, 0, 1024), (0, 1024, 1024),
+    (1, 0, 512), (1, 512, 512), (1, 1024, 512), (1, 1536, 256), (1, 1792, 256),
+)
 X_CHUNKS = (
-    (0, 0, 512, 416), (0, 512, 512, 416), (0, 1024, 512, 416), (0, 1536, 512, 416),
-    (1, 0, 512, 448), (1, 512, 512, 448), (1, 1024, 512, 448), (1, 1536, 256, 160), (1, 1792, 256, 96),
+    (0, 0, 512, 256), (0, 512, 512, 512),
+    (1, 1024, 512, 0), (1, 1536, 512, 384),
+    (2, 0, 512, 512),
+    (3, 512, 512, 384),
+    (4, 1024, 256, 0), (4, 1280, 256, 256),
+    (5, 1536, 256, 256),
+    (6, 1792, 256, 96),
 )
 
 
@@ -44,38 +57,47 @@ def tile_picked_hop2_relu_e_kernel(
             nc.sync.dma_start(held[:], dram)
             return held
 
-        def mx_tiles(name, width):
-            words = keep.tile([P, width], U32, name=name + "_words", align_bytes=64)
+        def mx_tiles(name, width, tag=""):
+            words = keep.tile([P, width], U32, name=name + "_words", align_bytes=64, tag=tag or name + "_words")
             scales = keep.tile([P, width], U8, name=name + "_scales", align_bytes=64)
             return words, scales
 
         def quantise(words, scales, grouped):
             nc.vector.quantize_mx(out=words.bitcast(FP8X4), scales=scales, in_=grouped)
 
-        x_all = [mx_tiles("x_all%d" % c, T) for c in range(PASSES)]
-        for c in range(PASSES):
-            nc.vector.memset(x_all[c][1][:].bitcast(I32), 0)
+        all_words = [keep.tile([P, T], U32, name="all_words%d" % c, align_bytes=64) for c in range(PASSES)]
+        all_scales = keep.tile([P, T], U8, name="all_scales", align_bytes=64)
+        nc.vector.memset(all_scales[:].bitcast(I32), 0)
+
+        identity = keep.tile([P, P], F32, name="identity")
+        make_identity(nc, identity[:])
 
         x_raw = []
-        for n, (c, first, width, share) in enumerate(X_CHUNKS):
+        for n, (c, first, width) in enumerate(X_LOADS):
             raw = keep.tile([P, PACK, width], F32, name="x_raw%d" % n)
             rows = xT[c * K_PASS : (c + 1) * K_PASS, first : first + width]
             nc.sync.dma_start(raw[:], rows.rearrange("(p j) w -> p j w", j=PACK))
             x_raw.append(raw)
-            if n == 2:
+            if n == 0:
                 offs_sb = load_list("offs_sb", offs)
         w1_raw = {}
         for c in range(PASSES):
-            for half in range(2):
-                raw = keep.tile([P, PACK, H // 2], F32, name="w1_raw%d%d" % (c, half))
-                rows = w1[c * K_PASS : (c + 1) * K_PASS, half * (H // 2) : (half + 1) * (H // 2)]
-                nc.sync.dma_start(raw[:], rows.rearrange("(p j) w -> p j w", j=PACK))
-                w1_raw[c, half] = raw
-        gate_sb = keep.tile([P, 2, V], F32, name="gate_sb")
-        nc.sync.dma_start(gate_sb[:], gate.rearrange("d p v -> p d v"))
+            raw = keep.tile([P, PACK, H], F32, name="w1_raw%d" % c)
+            nc.sync.dma_start(raw[:], w1[c * K_PASS : (c + 1) * K_PASS, :].rearrange("(p j) w -> p j w", j=PACK))
+            w1_raw[c] = raw
+        gate_early = []
+        for d in range(2):
+            held = keep.tile([P, TURNED * P], F32, name="gate_early%d" % d, tag="gate_early%d" % d)
+            nc.sync.dma_start(held[:], gate[d, :, : TURNED * P])
+            gate_early.append(held[:])
         pos_sb = [load_list("pos1_sb", pos1), load_list("pos2_sb", pos2)]
+        gate_rest = keep.tile([P, 2, V - TURNED * P], F32, name="gate_rest")
+        nc.sync.dma_start(gate_rest[:], gate[:, :, TURNED * P :].rearrange("d p v -> p d v"))
+        gate_late = [gate_rest[:, d, :] for d in range(2)]
         w2_raw = keep.tile([P, PACK, N], F32, name="w2_raw")
-        nc.sync.dma_start(w2_raw[:], w2.rearrange("(p j) w -> p j w", j=PACK))
+        w2_rows = w2.rearrange("(q t r) n -> r q t n", t=PACK, r=PACK)
+        for r in range(PACK):
+            nc.sync.dma_start(w2_raw[r:P:PACK, :, :], w2_rows[r])
         gate2_sb = keep.tile([P, 2, U], F32, name="gate2_sb")
         nc.sync.dma_start(gate2_sb[:], gate2.rearrange("d p v -> p d v"))
         nxt_sb = [load_list("nxt1_sb", nxt1), load_list("nxt2_sb", nxt2)]
@@ -86,110 +108,173 @@ def tile_picked_hop2_relu_e_kernel(
         def weave_in(ap):
             return ap.rearrange("p t (c i) -> p c t i", i=PACK)
 
-        def gather(sort, c, half, dtype, tag=""):
-            name = "picked%d%d%d" % (sort, c, half)
+        def gather(window, name, half, dtype, tag=""):
             held = keep.tile([P, BANK], dtype, name=name, align_bytes=64, tag=tag or name)
             picks = offs_sb[:, half * BANK // LIST_ROWS : (half + 1) * BANK // LIST_ROWS]
-            nc.vector.tensor_copy(held[:], x_all[c][sort][:].indirect(picks))
+            nc.vector.tensor_copy(held[:], window[:].indirect(picks))
             return held
 
-        picked = {}
-        for n, (c, first, width, share) in enumerate(X_CHUNKS):
+        picked_words = {}
+        picked_scales = {}
+
+        def round_chunk(n):
+            load, first, width, share = X_CHUNKS[n]
+            start = first - X_LOADS[load][1]
+            raw = x_raw[load][:, :, start : start + width]
             grouped = keep.tile([P, width, PACK], BF16, name="x_grouped%d" % n, align_bytes=64)
-            nc.scalar.activation(weave_out(grouped[:, :share, :]), weave_in(x_raw[n][:, :, :share]), COPY)
-            nc.vector.tensor_copy(weave_out(grouped[:, share:, :]), weave_in(x_raw[n][:, :, share:]))
+            if share > 0:
+                nc.scalar.activation(weave_out(grouped[:, :share, :]), weave_in(raw[:, :, :share]), COPY)
+            if share < width:
+                nc.vector.tensor_copy(weave_out(grouped[:, share:, :]), weave_in(raw[:, :, share:]))
+            return grouped
+
+        def quantise_chunk(n, grouped):
+            load, first, width, share = X_CHUNKS[n]
+            c = X_LOADS[load][0]
             quantise(
-                x_all[c][0][:, first : first + width],
-                x_all[c][1][:, first : first + width],
+                all_words[c][:, first : first + width],
+                all_scales[PLANE_STEP * c :, first : first + width],
                 grouped[:].rearrange("p w j -> p (w j)"),
             )
             if first + width == T:
+                if c == PASSES - 1:
+                    picked_scales[0] = gather(all_scales, "picked_scales0", 0, U8)
                 for half in range(2):
-                    words = gather(0, c, half, U32)
-                    if (c, half) == (PASSES - 1, 1):
-                        last_words = words
-                    else:
-                        picked[c, half] = (words, gather(1, c, half, U8))
+                    picked_words[c, half] = gather(all_words[c], "picked_words%d%d" % (c, half), half, U32)
+
+        pending = round_chunk(0)
+        for n in range(len(X_CHUNKS)):
+            ready = pending
+            if n + 1 < len(X_CHUNKS):
+                pending = round_chunk(n + 1)
+            quantise_chunk(n, ready)
 
         w1_q = {}
-        for c in range(PASSES):
-            grouped = keep.tile([P, PACK, P, PACK], BF16, name="w1_grouped%d" % c, align_bytes=64, tag="w1_grouped%d" % c)
-            for half in range(2):
-                nc.scalar.activation(
-                    grouped[:, :, half * (P // 2) : (half + 1) * (P // 2), :].rearrange("p t m j -> p m j t"),
-                    w1_raw[c, half][:].rearrange("p j (m t) -> p m j t", t=PACK),
-                    COPY,
-                )
-            words, scales = mx_tiles("w1_q%d" % c, H)
-            parts = ((0, 4),) if c == 0 else ((0, 1), (1, 2), (2, 4))
-            for lo, hi in parts:
-                quantise(
-                    words[:, lo * P : hi * P],
-                    scales[:, lo * P : hi * P],
-                    grouped[:, lo:hi, :, :].rearrange("p t m j -> p (t m j)"),
-                )
-            w1_q[c] = (words, scales)
-            if c == 0:
-                picked[PASSES - 1, 1] = (last_words, gather(1, PASSES - 1, 1, U8, tag="w1_grouped0"))
+
+        def prepare_w1(c, t, words, scales):
+            name = "w1_grouped%d%d" % (c, t)
+            grouped = keep.tile([P, P, PACK], BF16, name=name, align_bytes=64, tag=name)
+            columns = w1_raw[c][:].rearrange("p j (q t r) -> p t q j r", t=PACK, r=PACK)[:, t]
+            nc.scalar.activation(weave_out(grouped[:]), columns, COPY)
+            quantise(words, scales, grouped[:].rearrange("p w j -> p (w j)"))
+            w1_q[c, t] = (words, scales)
+
+        def prepare_alone(c, t):
+            words, scales = mx_tiles("w1_q%d%d" % (c, t), P)
+            prepare_w1(c, t, words[:], scales[:])
 
         def product(acc, left, cols, right, start, stop):
             nc.tensor.matmul_mx(
                 out=acc,
                 lhsT=left[0][:, cols].bitcast(FP8X4),
                 lhsT_scale=left[1][:, cols],
-                rhs=right[0][:].bitcast(FP8X4),
-                rhs_scale=right[1][:],
+                rhs=right[0].bitcast(FP8X4),
+                rhs_scale=right[1],
                 start=start,
                 stop=stop,
             )
+
+        def picked(c, half):
+            return picked_words[c, half][:], picked_scales[half][PLANE_STEP * c :, :]
 
         banks = {}
         for t in range(PACK):
             for half in range(2):
                 banks[t, half] = psum.tile([P, BANK], F32, name="h_bank%d%d" % (t, half), tag="bank%d" % (2 * t + half))
+
+        early = [keep.tile([P, PACK, TURNED * P], F32, name="early%d" % d) for d in range(2)]
+        late = [keep.tile([P, PACK, V - TURNED * P], F32, name="late%d" % d, tag="gate_early%d" % d) for d in range(2)]
+        h_tiles = []
+
+        def fetch_terms(terms, weights, t, lo, hi):
+            for d in range(2):
+                picks = pos_sb[d][:, lo // LIST_ROWS : hi // LIST_ROWS]
+                nc.vector.tensor_tensor(terms[d][:, t, :], h_tiles[t][:].indirect(picks), weights[d], MULT)
+
         for t in range(PACK):
+            if t == 0:
+                prepare_alone(0, t)
+                picked_scales[1] = gather(all_scales, "picked_scales1", 1, U8, tag="w1_grouped00")
+                prepare_alone(1, t)
+                words, scales = mx_tiles("w1_later", H - P, "w1_grouped10")
+                for later in range(1, PACK):
+                    cols = slice((later - 1) * P, later * P)
+                    prepare_w1(0, later, words[:, cols], scales[:, cols])
+                for later in range(1, PACK):
+                    prepare_alone(1, later)
             for c in range(PASSES):
                 for half in range(2):
-                    product(banks[t, half][:], w1_q[c], slice(t * P, (t + 1) * P), picked[c, half], c == 0, c == PASSES - 1)
-
-        w2_grouped = keep.tile([P, N, PACK], BF16, name="w2_grouped", align_bytes=64)
-        nc.vector.tensor_copy(weave_out(w2_grouped[:]), weave_in(w2_raw[:]))
-        w2_q = mx_tiles("w2_q", N)
-        quantise(w2_q[0][:], w2_q[1][:], w2_grouped[:].rearrange("p w j -> p (w j)"))
-
-        terms = [keep.tile([P, PACK, V], F32, name="terms%d" % d) for d in range(2)]
-        for t in range(PACK):
+                    product(banks[t, half][:], w1_q[c, t], slice(0, P), picked(c, half), c == 0, c == PASSES - 1)
             h = keep.tile([P, S], F32, name="h%d" % t)
             nc.scalar.activation(h[:, :BANK], banks[t, 0][:], RELU)
             if t == 0:
                 nc.vector.tensor_scalar_max(h[:, BANK:], banks[t, 1][:], 0.0)
             else:
                 nc.scalar.activation(h[:, BANK:], banks[t, 1][:], RELU)
-            for d in range(2):
-                nc.vector.tensor_tensor(terms[d][:, t, :], h[:].indirect(pos_sb[d][:]), gate_sb[:, d, :], MULT)
+            h_tiles.append(h)
+            fetch_terms(early, gate_early, t, 0, TURNED * P)
+        sums = [psum.tile([P, PACK, P], F32, name="sums%d" % b, tag="bank%d" % (4 + b)) for b in range(TURNED)]
+        for t in range(PACK):
+            for b in range(TURNED):
+                for d in range(2):
+                    nc.tensor.matmul(
+                        sums[b][:, t, :], early[d][:, t, b * P : (b + 1) * P], identity[:],
+                        start=(d == 0), stop=(d == 1), is_transpose=True,
+                    )
+        for t in range(PACK):
+            fetch_terms(late, gate_late, t, TURNED * P, V)
 
-        z_grouped = []
-        for half in range(2):
-            cols = slice(half * (V // 2), (half + 1) * (V // 2))
-            grouped = keep.tile([P, V // 2, PACK], BF16, name="z_grouped%d" % half, align_bytes=64)
-            nc.vector.tensor_tensor(weave_out(grouped[:]), weave_in(terms[0][:, :, cols]), weave_in(terms[1][:, :, cols]), ADD)
-            z_grouped.append(grouped)
+        w2_grouped = keep.tile([P, N, PACK], BF16, name="w2_grouped", align_bytes=64, tag="picked_words00")
+        nc.scalar.activation(weave_out(w2_grouped[:]), weave_in(w2_raw[:]), COPY)
+        w2_q = mx_tiles("w2_q", N)
+        quantise(w2_q[0][:], w2_q[1][:], w2_grouped[:].rearrange("p w j -> p (w j)"))
+
         g = [keep.tile([P, V], F32, name="g%d" % m) for m in range(N // P)]
+
+        z_grouped = keep.tile([P, V, PACK], BF16, name="z_grouped", align_bytes=64)
+        z_pairs = z_grouped[:].rearrange("p v t -> p (v t)").bitcast(F32).rearrange("p (v u) -> p v u", u=2)
+        back = psum.tile([P, TURNED, 2, P], F32, name="back", tag="bank0")
+        for b in range(TURNED):
+            turned = keep.tile([P, 2, P, 2], BF16, name="turned%d" % b)
+            nc.scalar.activation(turned[:], sums[b][:].rearrange("q (u e) p -> q u p e", e=2), COPY)
+            pairs = turned[:].rearrange("q u p e -> q (u p e)").bitcast(F32)
+            for u in range(2):
+                nc.tensor.transpose(back[:, b, u, :], pairs[:, u * P : (u + 1) * P], identity[:])
+        nc.scalar.copy(
+            z_pairs[:, : TURNED * P, :].rearrange("p (b q) u -> p b q u", b=TURNED),
+            back[:].rearrange("p b u q -> p b q u"),
+        )
+        nc.vector.tensor_tensor(weave_out(z_grouped[:, TURNED * P :, :]), weave_in(late[0][:]), weave_in(late[1][:]), ADD)
+
         z_q = []
         for half in range(2):
-            z_q.append(mx_tiles("z_q%d" % half, V // 2))
-            quantise(z_q[half][0][:], z_q[half][1][:], z_grouped[half][:].rearrange("p w j -> p (w j)"))
-        for half in range(2):
             cols = slice(half * (V // 2), (half + 1) * (V // 2))
-            for m in range(N // P):
-                acc = psum.tile([P, V // 2], F32, name="g_bank%d%d" % (m, half), tag="bank%d" % (2 * half + m))
-                product(acc[:], w2_q, slice(m * P, (m + 1) * P), z_q[half], True, True)
+            words, scales = mx_tiles("z_q%d" % half, V // 2)
+            quantise(words[:], scales[:], z_grouped[:, cols, :].rearrange("p w j -> p (w j)"))
+            z_q.append((words[:], scales[:]))
+        for m in range(N // P):
+            for half in range(2):
+                cols = slice(half * (V // 2), (half + 1) * (V // 2))
+                acc = psum.tile([P, V // 2], F32, name="g_bank%d%d" % (m, half), tag=G_BANKS[2 * m + half])
+                product(acc[:], (w2_q[0][:], w2_q[1][:]), slice(m * P, (m + 1) * P), z_q[half], True, True)
                 nc.scalar.activation(g[m][:, cols], acc[:], RELU)
 
         ends = [[keep.tile([P, U], F32, name="ends%d%d" % (m, d)) for d in range(2)] for m in range(N // P)]
-        for m in range(N // P):
-            for d in range(2):
-                nc.vector.tensor_tensor(ends[m][d][:], g[m][:].indirect(nxt_sb[d][:]), gate2_sb[:, d, :], MULT)
-            result = keep.tile([P, U], F32, name="result%d" % m)
-            nc.vector.tensor_tensor(result[:], ends[m][0][:], ends[m][1][:], ADD)
-            nc.sync.dma_start(out[m * P : (m + 1) * P, :], result[:])
+        result = [keep.tile([P, U], F32, name="result%d" % m) for m in range(N // P)]
+
+        def fetch(m, d, lo, hi):
+            picks = nxt_sb[d][:, lo // LIST_ROWS : hi // LIST_ROWS]
+            nc.vector.tensor_tensor(ends[m][d][:, lo:hi], g[m][:].indirect(picks), gate2_sb[:, d, lo:hi], MULT)
+
+        def finish(m, lo, hi, queue):
+            nc.vector.tensor_tensor(result[m][:, lo:hi], ends[m][0][:, lo:hi], ends[m][1][:, lo:hi], ADD)
+            queue.dma_start(out[m * P : (m + 1) * P, lo:hi], result[m][:, lo:hi])
+
+        fetch(0, 0, 0, U)
+        fetch(0, 1, 0, U)
+        fetch(1, 0, 0, U)
+        finish(0, 0, U, nc.sync)
+        fetch(1, 1, 0, U // 2)
+        fetch(1, 1, U // 2, U)
+        finish(1, 0, U // 2, nc.scalar)
+        finish(1, U // 2, U, nc.sync)

@@ -25,6 +25,7 @@ PASSES = K // K_PASS
 BANK = 512
 LIST_ROWS = 16
 PLANE_STEP = 4
+WARM_PASSES = 4
 TURNED = 2
 G_BANKS = ("bank1", "bank2", "bank3", "bank6")
 
@@ -176,6 +177,10 @@ def tile_picked_hop2_relu_e_kernel(
 
         def picked(c, half):
             return picked_words[c, half][:], picked_scales[half][PLANE_STEP * c :, :]
+
+        warm = psum.tile([P, BANK], F32, name="warm", tag="bank7")
+        for n in range(WARM_PASSES):
+            product(warm[:], picked(0, 0), slice(0, P), picked(0, 0), True, True)
 
         banks = {}
         for t in range(PACK):

from contextlib import ExitStack

import concourse.mybir as mybir
from concourse.masks import make_identity

K, T, S, V, H, N, U = 1024, 2048, 1024, 512, 512, 256, 256
FLOPS = 2 * K * H * S + 2 * H * N * V

F32 = mybir.dt.float32
BF16 = mybir.dt.bfloat16
I32 = mybir.dt.int32
U32 = mybir.dt.uint32
U16 = mybir.dt.uint16
U8 = mybir.dt.uint8
FP8X4 = mybir.dt.float8_e4m3fn_x4
COPY = mybir.ActivationFunctionType.Copy
RELU = mybir.ActivationFunctionType.Relu
MULT = mybir.AluOpType.mult
ADD = mybir.AluOpType.add

P = 128
PACK = 4
K_PASS = P * PACK
PASSES = K // K_PASS
BANK = 512
LIST_ROWS = 16
PLANE_STEP = 4
WARM_PASSES = 4
TURNED = 2
G_BANKS = ("bank1", "bank2", "bank3", "bank6")

X_LOADS = (
    (0, 0, 1024), (0, 1024, 1024),
    (1, 0, 512), (1, 512, 512), (1, 1024, 512), (1, 1536, 256), (1, 1792, 256),
)
X_CHUNKS = (
    (0, 0, 512, 256), (0, 512, 512, 512),
    (1, 1024, 512, 0), (1, 1536, 512, 384),
    (2, 0, 512, 512),
    (3, 512, 512, 384),
    (4, 1024, 256, 0), (4, 1280, 256, 256),
    (5, 1536, 256, 256),
    (6, 1792, 256, 96),
)


def tile_picked_hop2_relu_e_kernel(
    tc, xT, w1, w2, gate, gate2, offs, pos1, pos2, nxt1, nxt2, out
):
    nc = tc.nc
    with ExitStack() as ctx:
        lists = ctx.enter_context(tc.tile_pool(name="lists", bufs=1))
        keep = ctx.enter_context(tc.tile_pool(name="keep", bufs=1))
        psum = ctx.enter_context(tc.psum_pool(name="psum", bufs=1))

        def load_list(name, dram):
            held = lists.tile(list(dram.shape), U16, name=name)
            nc.sync.dma_start(held[:], dram)
            return held

        def mx_tiles(name, width, tag=""):
            words = keep.tile([P, width], U32, name=name + "_words", align_bytes=64, tag=tag or name + "_words")
            scales = keep.tile([P, width], U8, name=name + "_scales", align_bytes=64)
            return words, scales

        def quantise(words, scales, grouped):
            nc.vector.quantize_mx(out=words.bitcast(FP8X4), scales=scales, in_=grouped)

        all_words = [keep.tile([P, T], U32, name="all_words%d" % c, align_bytes=64) for c in range(PASSES)]
        all_scales = keep.tile([P, T], U8, name="all_scales", align_bytes=64)
        nc.vector.memset(all_scales[:].bitcast(I32), 0)

        identity = keep.tile([P, P], F32, name="identity")
        make_identity(nc, identity[:])

        x_raw = []
        for n, (c, first, width) in enumerate(X_LOADS):
            raw = keep.tile([P, PACK, width], F32, name="x_raw%d" % n)
            rows = xT[c * K_PASS : (c + 1) * K_PASS, first : first + width]
            nc.sync.dma_start(raw[:], rows.rearrange("(p j) w -> p j w", j=PACK))
            x_raw.append(raw)
            if n == 0:
                offs_sb = load_list("offs_sb", offs)
        w1_raw = {}
        for c in range(PASSES):
            raw = keep.tile([P, PACK, H], F32, name="w1_raw%d" % c)
            nc.sync.dma_start(raw[:], w1[c * K_PASS : (c + 1) * K_PASS, :].rearrange("(p j) w -> p j w", j=PACK))
            w1_raw[c] = raw
        gate_early = []
        for d in range(2):
            held = keep.tile([P, TURNED * P], F32, name="gate_early%d" % d, tag="gate_early%d" % d)
            nc.sync.dma_start(held[:], gate[d, :, : TURNED * P])
            gate_early.append(held[:])
        pos_sb = [load_list("pos1_sb", pos1), load_list("pos2_sb", pos2)]
        gate_rest = keep.tile([P, 2, V - TURNED * P], F32, name="gate_rest")
        nc.sync.dma_start(gate_rest[:], gate[:, :, TURNED * P :].rearrange("d p v -> p d v"))
        gate_late = [gate_rest[:, d, :] for d in range(2)]
        w2_raw = keep.tile([P, PACK, N], F32, name="w2_raw")
        w2_rows = w2.rearrange("(q t r) n -> r q t n", t=PACK, r=PACK)
        for r in range(PACK):
            nc.sync.dma_start(w2_raw[r:P:PACK, :, :], w2_rows[r])
        gate2_sb = keep.tile([P, 2, U], F32, name="gate2_sb")
        nc.sync.dma_start(gate2_sb[:], gate2.rearrange("d p v -> p d v"))
        nxt_sb = [load_list("nxt1_sb", nxt1), load_list("nxt2_sb", nxt2)]

        def weave_out(ap):
            return ap.rearrange("p (c i) t -> p c t i", i=PACK)

        def weave_in(ap):
            return ap.rearrange("p t (c i) -> p c t i", i=PACK)

        def gather(window, name, half, dtype, tag=""):
            held = keep.tile([P, BANK], dtype, name=name, align_bytes=64, tag=tag or name)
            picks = offs_sb[:, half * BANK // LIST_ROWS : (half + 1) * BANK // LIST_ROWS]
            nc.vector.tensor_copy(held[:], window[:].indirect(picks))
            return held

        picked_words = {}
        picked_scales = {}

        def round_chunk(n):
            load, first, width, share = X_CHUNKS[n]
            start = first - X_LOADS[load][1]
            raw = x_raw[load][:, :, start : start + width]
            grouped = keep.tile([P, width, PACK], BF16, name="x_grouped%d" % n, align_bytes=64)
            if share > 0:
                nc.scalar.activation(weave_out(grouped[:, :share, :]), weave_in(raw[:, :, :share]), COPY)
            if share < width:
                nc.vector.tensor_copy(weave_out(grouped[:, share:, :]), weave_in(raw[:, :, share:]))
            return grouped

        def quantise_chunk(n, grouped):
            load, first, width, share = X_CHUNKS[n]
            c = X_LOADS[load][0]
            quantise(
                all_words[c][:, first : first + width],
                all_scales[PLANE_STEP * c :, first : first + width],
                grouped[:].rearrange("p w j -> p (w j)"),
            )
            if first + width == T:
                if c == PASSES - 1:
                    picked_scales[0] = gather(all_scales, "picked_scales0", 0, U8)
                for half in range(2):
                    picked_words[c, half] = gather(all_words[c], "picked_words%d%d" % (c, half), half, U32)

        pending = round_chunk(0)
        for n in range(len(X_CHUNKS)):
            ready = pending
            if n + 1 < len(X_CHUNKS):
                pending = round_chunk(n + 1)
            quantise_chunk(n, ready)

        w1_q = {}

        def prepare_w1(c, t, words, scales):
            name = "w1_grouped%d%d" % (c, t)
            grouped = keep.tile([P, P, PACK], BF16, name=name, align_bytes=64, tag=name)
            columns = w1_raw[c][:].rearrange("p j (q t r) -> p t q j r", t=PACK, r=PACK)[:, t]
            nc.scalar.activation(weave_out(grouped[:]), columns, COPY)
            quantise(words, scales, grouped[:].rearrange("p w j -> p (w j)"))
            w1_q[c, t] = (words, scales)

        def prepare_alone(c, t):
            words, scales = mx_tiles("w1_q%d%d" % (c, t), P)
            prepare_w1(c, t, words[:], scales[:])

        def product(acc, left, cols, right, start, stop):
            nc.tensor.matmul_mx(
                out=acc,
                lhsT=left[0][:, cols].bitcast(FP8X4),
                lhsT_scale=left[1][:, cols],
                rhs=right[0].bitcast(FP8X4),
                rhs_scale=right[1],
                start=start,
                stop=stop,
            )

        def picked(c, half):
            return picked_words[c, half][:], picked_scales[half][PLANE_STEP * c :, :]

        warm = psum.tile([P, BANK], F32, name="warm", tag="bank7")
        for n in range(WARM_PASSES):
            product(warm[:], picked(0, 0), slice(0, P), picked(0, 0), True, True)

        banks = {}
        for t in range(PACK):
            for half in range(2):
                banks[t, half] = psum.tile([P, BANK], F32, name="h_bank%d%d" % (t, half), tag="bank%d" % (2 * t + half))

        early = [keep.tile([P, PACK, TURNED * P], F32, name="early%d" % d) for d in range(2)]
        late = [keep.tile([P, PACK, V - TURNED * P], F32, name="late%d" % d, tag="gate_early%d" % d) for d in range(2)]
        h_tiles = []

        def fetch_terms(terms, weights, t, lo, hi):
            for d in range(2):
                picks = pos_sb[d][:, lo // LIST_ROWS : hi // LIST_ROWS]
                nc.vector.tensor_tensor(terms[d][:, t, :], h_tiles[t][:].indirect(picks), weights[d], MULT)

        for t in range(PACK):
            if t == 0:
                prepare_alone(0, t)
                picked_scales[1] = gather(all_scales, "picked_scales1", 1, U8, tag="w1_grouped00")
                prepare_alone(1, t)
                words, scales = mx_tiles("w1_later", H - P, "w1_grouped10")
                for later in range(1, PACK):
                    cols = slice((later - 1) * P, later * P)
                    prepare_w1(0, later, words[:, cols], scales[:, cols])
                for later in range(1, PACK):
                    prepare_alone(1, later)
            for c in range(PASSES):
                for half in range(2):
                    product(banks[t, half][:], w1_q[c, t], slice(0, P), picked(c, half), c == 0, c == PASSES - 1)
            h = keep.tile([P, S], F32, name="h%d" % t)
            nc.scalar.activation(h[:, :BANK], banks[t, 0][:], RELU)
            if t == 0:
                nc.vector.tensor_scalar_max(h[:, BANK:], banks[t, 1][:], 0.0)
            else:
                nc.scalar.activation(h[:, BANK:], banks[t, 1][:], RELU)
            h_tiles.append(h)
            fetch_terms(early, gate_early, t, 0, TURNED * P)
        sums = [psum.tile([P, PACK, P], F32, name="sums%d" % b, tag="bank%d" % (4 + b)) for b in range(TURNED)]
        for t in range(PACK):
            for b in range(TURNED):
                for d in range(2):
                    nc.tensor.matmul(
                        sums[b][:, t, :], early[d][:, t, b * P : (b + 1) * P], identity[:],
                        start=(d == 0), stop=(d == 1), is_transpose=True,
                    )
        for t in range(PACK):
            fetch_terms(late, gate_late, t, TURNED * P, V)

        w2_grouped = keep.tile([P, N, PACK], BF16, name="w2_grouped", align_bytes=64, tag="picked_words00")
        nc.scalar.activation(weave_out(w2_grouped[:]), weave_in(w2_raw[:]), COPY)
        w2_q = mx_tiles("w2_q", N)
        quantise(w2_q[0][:], w2_q[1][:], w2_grouped[:].rearrange("p w j -> p (w j)"))

        g = [keep.tile([P, V], F32, name="g%d" % m) for m in range(N // P)]

        z_grouped = keep.tile([P, V, PACK], BF16, name="z_grouped", align_bytes=64)
        z_pairs = z_grouped[:].rearrange("p v t -> p (v t)").bitcast(F32).rearrange("p (v u) -> p v u", u=2)
        back = psum.tile([P, TURNED, 2, P], F32, name="back", tag="bank0")
        for b in range(TURNED):
            turned = keep.tile([P, 2, P, 2], BF16, name="turned%d" % b)
            nc.scalar.activation(turned[:], sums[b][:].rearrange("q (u e) p -> q u p e", e=2), COPY)
            pairs = turned[:].rearrange("q u p e -> q (u p e)").bitcast(F32)
            for u in range(2):
                nc.tensor.transpose(back[:, b, u, :], pairs[:, u * P : (u + 1) * P], identity[:])
        nc.scalar.copy(
            z_pairs[:, : TURNED * P, :].rearrange("p (b q) u -> p b q u", b=TURNED),
            back[:].rearrange("p b u q -> p b q u"),
        )
        nc.vector.tensor_tensor(weave_out(z_grouped[:, TURNED * P :, :]), weave_in(late[0][:]), weave_in(late[1][:]), ADD)

        z_q = []
        for half in range(2):
            cols = slice(half * (V // 2), (half + 1) * (V // 2))
            words, scales = mx_tiles("z_q%d" % half, V // 2)
            quantise(words[:], scales[:], z_grouped[:, cols, :].rearrange("p w j -> p (w j)"))
            z_q.append((words[:], scales[:]))
        for m in range(N // P):
            for half in range(2):
                cols = slice(half * (V // 2), (half + 1) * (V // 2))
                acc = psum.tile([P, V // 2], F32, name="g_bank%d%d" % (m, half), tag=G_BANKS[2 * m + half])
                product(acc[:], (w2_q[0][:], w2_q[1][:]), slice(m * P, (m + 1) * P), z_q[half], True, True)
                nc.scalar.activation(g[m][:, cols], acc[:], RELU)

        ends = [[keep.tile([P, U], F32, name="ends%d%d" % (m, d)) for d in range(2)] for m in range(N // P)]
        result = [keep.tile([P, U], F32, name="result%d" % m) for m in range(N // P)]

        def fetch(m, d, lo, hi):
            picks = nxt_sb[d][:, lo // LIST_ROWS : hi // LIST_ROWS]
            nc.vector.tensor_tensor(ends[m][d][:, lo:hi], g[m][:].indirect(picks), gate2_sb[:, d, lo:hi], MULT)

        def finish(m, lo, hi, queue):
            nc.vector.tensor_tensor(result[m][:, lo:hi], ends[m][0][:, lo:hi], ends[m][1][:, lo:hi], ADD)
            queue.dma_start(out[m * P : (m + 1) * P, lo:hi], result[m][:, lo:hi])

        fetch(0, 0, 0, U)
        fetch(0, 1, 0, U)
        fetch(1, 0, 0, U)
        finish(0, 0, U, nc.sync)
        fetch(1, 1, 0, U // 2)
        fetch(1, 1, U // 2, U)
        finish(1, 0, U // 2, nc.scalar)
        finish(1, U // 2, U, nc.sync)
